import numpy as np
import ml_dtypes


def mxq(x, axis, fmt="e4m3"):
    dtype, down = {"e4m3": (ml_dtypes.float8_e4m3fn, 7), "e5m2": (ml_dtypes.float8_e5m2, 14)}[fmt]
    v = np.moveaxis(np.asarray(x, np.float32).astype(ml_dtypes.bfloat16).astype(np.float64), axis, -1)
    blocks = v.reshape(v.shape[:-1] + (-1, 32))
    amax = np.abs(blocks).max(-1, keepdims=True)
    byte = np.maximum(np.where(amax > 0, np.frexp(amax)[1] - 1 + 127, 0) - down, 1)
    scale = np.exp2(byte - 127.0)
    codes = (blocks / scale).astype(np.float32).astype(dtype).astype(np.float64)
    return np.moveaxis((codes * scale).reshape(v.shape), -1, axis)


WIDE = False


def mx_kscale(k):
    if not WIDE:
        return np.ones(k)
    levels = np.array([10, -10, 5, -5, 0])
    if k % 512:
        return np.exp2(np.random.permutation(np.resize(levels, k // 32))).repeat(32)
    a = np.empty((k // 512, 16))
    for p in range(k // 512):
        a[p, :8] = np.random.permutation(np.resize(levels, 8))
        for g in range(8):
            far = levels[np.abs(levels - a[p, g]) >= 10]
            a[p, g + 8] = far[np.random.randint(len(far))]
    return np.exp2(a.ravel()).repeat(32)


def f64(x):
    return np.asarray(x).astype(np.float64)


def striped8(idx):
    return np.asarray(idx).reshape(8, -1, 16).transpose(0, 2, 1).reshape(128, -1).astype(np.uint16)


def unstriped8(offs):
    return offs.reshape(8, 16, -1).transpose(0, 2, 1).reshape(8, -1).astype(np.int64)


def pick8(x, idx, run):
    r = np.arange(len(x))
    return x[r[:, None], idx[r % (8 * run) // run]]


E2M1 = np.array([0.0, 0.5, 1.0, 1.5, 2.0, 3.0, 4.0, 6.0, -0.0, -0.5, -1.0, -1.5, -2.0, -3.0, -4.0, -6.0])


def pack_weight(w, fmt):
    k, n = w.shape
    w = f64(np.asarray(w, np.float32).astype(ml_dtypes.bfloat16)).reshape(k // 32, 32, n)
    amax = np.abs(w).max(1)
    if fmt == "e4m3":
        byte = np.frexp(amax)[1] - 1 + 127 - 7
    else:
        mant, ex = np.frexp(amax / 6.0)
        byte = np.where(mant > 0.5, ex, ex - 1) + 127
    byte = np.clip(np.where(amax > 0, byte, 1), 1, 254)
    scaled = (w * np.exp2(127.0 - byte)[:, None, :]).reshape(k, n).astype(np.float32)
    by_word = np.ascontiguousarray(scaled.reshape(k // 512, 128, 4, n).transpose(0, 1, 3, 2))
    if fmt == "e4m3":
        words = by_word.astype(ml_dtypes.float8_e4m3fn).view(np.uint8)
    else:
        c = by_word.astype(ml_dtypes.float4_e2m1fn).view(np.uint8) & 0xF
        words = (c[..., 0::2] | (c[..., 1::2] << 4)).reshape(k // 512, 128, 2 * n)
    return np.ascontiguousarray(words), np.ascontiguousarray(byte.astype(np.uint8).reshape(k // 512, 16, n))


def unpack_weight(words, scales, fmt):
    g, _, n = scales.shape
    words = np.ascontiguousarray(words).reshape(g, 128, n, -1)
    if fmt == "e4m3":
        vals = words.view(ml_dtypes.float8_e4m3fn).astype(np.float64)
    else:
        nib = np.empty((g, 128, n, 4), np.uint8)
        nib[..., 0::2] = words & 0xF
        nib[..., 1::2] = words >> 4
        vals = E2M1[nib]
    vals = vals * np.repeat(np.exp2(scales.astype(np.float64) - 127.0), 8, axis=1)[..., None]
    return vals.transpose(0, 1, 3, 2).reshape(g * 512, n)


def sigmoid(v):
    return 1.0 / (1.0 + np.exp(-v))


D, T, I, Q = 512, 1024, 512, 128


def setup_inputs():
    n = np.random.standard_normal
    idx = np.stack([np.random.permutation(T)[:I] for _ in range(8)])
    idx2 = np.stack([np.random.permutation(T)[:I] for _ in range(8)])
    idx3 = np.stack([np.random.permutation(T)[:I] for _ in range(8)])
    idx4 = np.stack([np.random.permutation(T)[:I] for _ in range(8)])
    fd = mx_kscale(D)
    keysp = pack_weight(n((D, T)) / fd[:, None], "e4m3")
    tagsp = pack_weight(n((D, T)) / fd[:, None], "e2m1")
    return {
        "query": (n((D, Q)) * 0.75 / np.sqrt(D) * fd[:, None]).astype(np.float32),
        "query2": (n((D, Q)) * 0.75 / np.sqrt(D) * fd[:, None]).astype(np.float32),
        "keys_words": keysp[0],
        "keys_scales": keysp[1],
        "tags_words": tagsp[0],
        "tags_scales": tagsp[1],
        "thr": (np.random.uniform(-0.6, 0.6, (Q, 1))).astype(np.float32),
        "slope": (np.random.uniform(1.0, 3.0, (Q, 1))).astype(np.float32),
        "offs": striped8(idx),
        "offs2": striped8(idx2),
        "offs3": striped8(idx3),
        "offs4": striped8(idx4),
    }


def reference(query, query2, keys_words, keys_scales, tags_words, tags_scales, thr, slope, offs, offs2, offs3, offs4):
    idx = unstriped8(offs)
    idx2 = unstriped8(offs2)
    idx3 = unstriped8(offs3)
    idx4 = unstriped8(offs4)
    keysu = unpack_weight(keys_words, keys_scales, "e4m3")
    tagsu = unpack_weight(tags_words, tags_scales, "e2m1")
    queryq = mxq(f64(query), 0, "e4m3")
    query2q = mxq(f64(query2), 0, "e4m3")
    a = queryq.T @ keysu + query2q.T @ tagsu
    f1 = np.zeros((Q, T))
    f1[np.arange(Q)[:, None], idx2[np.arange(Q) % 128 // 16]] = pick8(a, idx, 16)
    cc = a + f1
    s1 = sigmoid(pick8(cc, idx3, 16) * f64(slope) + f64(thr))
    f2 = np.zeros((Q, T))
    f2[np.arange(Q)[:, None], idx[np.arange(Q) % 128 // 16]] = s1
    dd = cc - f2 * 2.0
    y = pick8(dd, idx4, 16)
    return y

@@ -1,0 +1,117 @@
+from contextlib import ExitStack
+
+import concourse.mybir as mybir
+
+F32 = mybir.dt.float32
+BF16 = mybir.dt.bfloat16
+I32 = mybir.dt.int32
+U32 = mybir.dt.uint32
+U16 = mybir.dt.uint16
+U8 = mybir.dt.uint8
+FP8X4 = mybir.dt.float8_e4m3fn_x4
+FP4X4 = mybir.dt.float4_e2m1fn_x4
+ALU = mybir.AluOpType
+ACT = mybir.ActivationFunctionType
+
+P = 128
+PACK = 4
+D, T, I, Q = 512, 1024, 512, 128
+BANK = 512
+HALF = I // 2
+HALF_COLS = HALF // 16
+
+FLOPS = 2 * 2 * D * Q * T
+
+
+def tile_attend_opengate_parts_kernel(tc, query, query2, keys_words, keys_scales, tags_words, tags_scales,
+                                       thr, slope, offs, offs2, offs3, offs4, out):
+    nc = tc.nc
+    with ExitStack() as ctx:
+        sb = ctx.enter_context(tc.tile_pool(name="sb", bufs=1))
+        psum = ctx.enter_context(tc.psum_pool(name="psum", bufs=1))
+
+        key_scale = sb.tile([P, T], U8, align_bytes=64)
+        tag_scale = sb.tile([P, T], U8, align_bytes=64)
+        nc.vector.memset(tag_scale[:].bitcast(I32), 0)
+        nc.vector.memset(key_scale[:].bitcast(I32), 0)
+        f1 = sb.tile([P, T], F32)
+        f2 = sb.tile([P, T], F32)
+        nc.vector.memset(f1[:], 0.0)
+        nc.vector.memset(f2[:], 0.0)
+
+        raw = [sb.tile([P, PACK, Q], F32, name="raw%d" % u) for u in range(2)]
+        key_words = [sb.tile([P, BANK], U32, align_bytes=64, name="key_words%d" % h) for h in range(2)]
+        tag_words = sb.tile([P, 2 * T], U8, align_bytes=64)
+        lists = [sb.tile([P, I // 16], U16, name="list%d" % u) for u in range(4)]
+        thr_sb = sb.tile([P, 1], F32)
+        slope_sb = sb.tile([P, 1], F32)
+
+        def scale_rows(eng, plane, src, quad):
+            eng.dma_start(out=plane[32 * quad:32 * quad + 4, :].bitcast(I32), in_=src[0, 4 * quad:4 * quad + 4, :].bitcast(I32))
+
+        nc.sync.dma_start(out=raw[1][:], in_=query2.rearrange("(p j) c -> p j c", j=PACK))
+        nc.sync.dma_start(out=tag_words[:].bitcast(I32), in_=tags_words[0].bitcast(I32))
+        for quad in range(4):
+            scale_rows(nc.sync, tag_scale, tags_scales, quad)
+        nc.sync.dma_start(out=raw[0][:], in_=query.rearrange("(p j) c -> p j c", j=PACK))
+        key_src = keys_words[0].rearrange("p n t -> p (n t)").bitcast(I32)
+        for h in range(2):
+            nc.sync.dma_start(out=key_words[h][:].bitcast(I32), in_=key_src[:, h * BANK:(h + 1) * BANK])
+        for quad in range(4):
+            scale_rows(nc.scalar, key_scale, keys_scales, quad)
+        for tile, src in zip(lists, (offs, offs2, offs3, offs4)):
+            nc.sync.dma_start(tile[:], src)
+        nc.gpsimd.dma_start(out=thr_sb[:], in_=thr)
+        nc.gpsimd.dma_start(out=slope_sb[:], in_=slope)
+
+        codes = {}
+        scales = {}
+        for u in (1, 0):
+            grouped = sb.tile([P, Q, PACK], BF16, align_bytes=64, name="grouped%d" % u)
+            nc.vector.tensor_copy(out=grouped[:].rearrange("p (c i) t -> p c t i", i=4),
+                                  in_=raw[u][:].rearrange("p t (c i) -> p c t i", i=4))
+            q_codes = sb.tile([P, Q], U32, align_bytes=64, name="q_codes%d" % u)
+            q_scale = sb.tile([P, Q], U8, align_bytes=64, name="q_scale%d" % u)
+            nc.vector.quantize_mx(out=q_codes[:].bitcast(FP8X4), scales=q_scale[:], in_=grouped[:].rearrange("p c t -> p (c t)"))
+            codes[u] = q_codes
+            scales[u] = q_scale
+
+        spans = [(0, 512), (512, 768), (768, 1024)]
+        banks = [psum.tile([P, hi - lo], F32, name="bank%d" % lo) for lo, hi in spans]
+        for bank, (lo, hi) in zip(banks, spans):
+            nc.tensor.matmul_mx(out=bank[:], lhsT=codes[1][:].bitcast(FP8X4), lhsT_scale=scales[1][:],
+                                rhs=tag_words[:, 2 * lo:2 * hi].bitcast(FP4X4), rhs_scale=tag_scale[:, lo:hi],
+                                start=True, stop=False)
+        for bank, (lo, hi) in zip(banks, spans):
+            h = lo // BANK
+            nc.tensor.matmul_mx(out=bank[:], lhsT=codes[0][:].bitcast(FP8X4), lhsT_scale=scales[0][:],
+                                rhs=key_words[h][:, lo - h * BANK:hi - h * BANK].bitcast(FP8X4), rhs_scale=key_scale[:, lo:hi],
+                                start=False, stop=True)
+
+        a = sb.tile([P, T], F32)
+        nc.scalar.copy(out=a[:, :512], in_=banks[0][:])
+        nc.vector.tensor_copy(out=a[:, 512:768], in_=banks[1][:])
+        nc.vector.tensor_copy(out=a[:, 768:], in_=banks[2][:])
+
+        halves = [slice(h * HALF_COLS, (h + 1) * HALF_COLS) for h in range(2)]
+        picked = sb.tile([P, I], F32)
+        nc.vector.tensor_copy(out=picked[:, :HALF], in_=a[:].indirect(lists[0][:, halves[0]]))
+        nc.scalar.activation(out=picked[:, HALF:], in_=a[:].indirect(lists[0][:, halves[1]]), func=ACT.Copy)
+        nc.vector.tensor_copy(out=f1[:].indirect(lists[1][:]), in_=picked[:])
+        cc = sb.tile([P, T], F32)
+        nc.vector.tensor_tensor(out=cc[:], in0=a[:], in1=f1[:], op=ALU.add)
+
+        gate = [sb.tile([P, HALF], F32, name="gate%d" % h) for h in range(2)]
+        for h in range(2):
+            nc.scalar.activation(out=gate[h][:], in_=cc[:].indirect(lists[2][:, halves[h]]), func=ACT.Sigmoid,
+                                 bias=thr_sb[:], scale=slope_sb[:])
+        for h in range(2):
+            nc.vector.tensor_copy(out=f2[:].indirect(lists[0][:, halves[h]]), in_=gate[h][:])
+        dd = sb.tile([P, T], F32)
+        nc.vector.scalar_tensor_tensor(out=dd[:], in0=f2[:], scalar=-2.0, in1=cc[:], op0=ALU.mult, op1=ALU.add)
+
+        result = [sb.tile([P, HALF], F32, name="result%d" % h) for h in range(2)]
+        nc.vector.tensor_copy(out=result[0][:], in_=dd[:].indirect(lists[3][:, halves[0]]))
+        nc.scalar.activation(out=result[1][:], in_=dd[:].indirect(lists[3][:, halves[1]]), func=ACT.Copy)
+        nc.sync.dma_start(out=out[:, :HALF], in_=result[0][:])
+        nc.scalar.dma_start(out=out[:, HALF:], in_=result[1][:])

@@ -32,8 +32,6 @@ def tile_attend_opengate_parts_kernel(tc, query, query2, keys_words, keys_scales
 
         key_scale = sb.tile([P, T], U8, align_bytes=64)
         tag_scale = sb.tile([P, T], U8, align_bytes=64)
-        nc.vector.memset(tag_scale[:].bitcast(I32), 0)
-        nc.vector.memset(key_scale[:].bitcast(I32), 0)
         f1 = sb.tile([P, T], F32)
         f2 = sb.tile([P, T], F32)
         nc.vector.memset(f1[:], 0.0)
@@ -50,19 +48,19 @@ def tile_attend_opengate_parts_kernel(tc, query, query2, keys_words, keys_scales
             eng.dma_start(out=plane[32 * quad:32 * quad + 4, :].bitcast(I32), in_=src[0, 4 * quad:4 * quad + 4, :].bitcast(I32))
 
         nc.sync.dma_start(out=raw[1][:], in_=query2.rearrange("(p j) c -> p j c", j=PACK))
-        nc.sync.dma_start(out=tag_words[:].bitcast(I32), in_=tags_words[0].bitcast(I32))
         for quad in range(4):
             scale_rows(nc.sync, tag_scale, tags_scales, quad)
+        nc.sync.dma_start(out=tag_words[:].bitcast(I32), in_=tags_words[0].bitcast(I32))
         nc.sync.dma_start(out=raw[0][:], in_=query.rearrange("(p j) c -> p j c", j=PACK))
         key_src = keys_words[0].rearrange("p n t -> p (n t)").bitcast(I32)
-        for h in range(2):
-            nc.sync.dma_start(out=key_words[h][:].bitcast(I32), in_=key_src[:, h * BANK:(h + 1) * BANK])
+        nc.sync.dma_start(out=key_words[0][:].bitcast(I32), in_=key_src[:, :BANK])
         for quad in range(4):
-            scale_rows(nc.scalar, key_scale, keys_scales, quad)
+            scale_rows(nc.sync, key_scale, keys_scales, quad)
+        nc.sync.dma_start(out=key_words[1][:].bitcast(I32), in_=key_src[:, BANK:])
         for tile, src in zip(lists, (offs, offs2, offs3, offs4)):
             nc.sync.dma_start(tile[:], src)
-        nc.gpsimd.dma_start(out=thr_sb[:], in_=thr)
-        nc.gpsimd.dma_start(out=slope_sb[:], in_=slope)
+        nc.sync.dma_start(out=thr_sb[:], in_=thr)
+        nc.sync.dma_start(out=slope_sb[:], in_=slope)
 
         codes = {}
         scales = {}

@@ -37,6 +37,10 @@ def tile_attend_opengate_parts_kernel(tc, query, query2, keys_words, keys_scales
         nc.vector.memset(f1[:], 0.0)
         nc.vector.memset(f2[:], 0.0)
 
+        warm_in = sb.tile([P, 1], F32)
+        warm_out = sb.tile([P, 1], F32)
+        nc.gpsimd.memset(warm_in[:], 0.0)
+        nc.scalar.activation(out=warm_out[:], in_=warm_in[:], func=ACT.Sigmoid)
         raw = [sb.tile([P, PACK, Q], F32, name="raw%d" % u) for u in range(2)]
         key_words = [sb.tile([P, BANK], U32, align_bytes=64, name="key_words%d" % h) for h in range(2)]
         tag_words = sb.tile([P, 2 * T], U8, align_bytes=64)
@@ -97,7 +101,9 @@ def tile_attend_opengate_parts_kernel(tc, query, query2, keys_words, keys_scales
         nc.scalar.activation(out=picked[:, HALF:], in_=a[:].indirect(lists[0][:, halves[1]]), func=ACT.Copy)
         nc.vector.tensor_copy(out=f1[:].indirect(lists[1][:]), in_=picked[:])
         cc = sb.tile([P, T], F32)
-        nc.vector.tensor_tensor(out=cc[:], in0=a[:], in1=f1[:], op=ALU.add)
+        nc.gpsimd.tensor_tensor(out=cc[:, 704:], in0=a[:, 704:], in1=f1[:, 704:], op=ALU.add)
+        nc.vector.tensor_tensor(out=cc[:, :512], in0=banks[0][:], in1=f1[:, :512], op=ALU.add)
+        nc.vector.tensor_tensor(out=cc[:, 512:704], in0=banks[1][:, :192], in1=f1[:, 512:704], op=ALU.add)
 
         gate = [sb.tile([P, HALF], F32, name="gate%d" % h) for h in range(2)]
         for h in range(2):

from contextlib import ExitStack

import concourse.mybir as mybir

F32 = mybir.dt.float32
BF16 = mybir.dt.bfloat16
I32 = mybir.dt.int32
U32 = mybir.dt.uint32
U16 = mybir.dt.uint16
U8 = mybir.dt.uint8
FP8X4 = mybir.dt.float8_e4m3fn_x4
FP4X4 = mybir.dt.float4_e2m1fn_x4
ALU = mybir.AluOpType
ACT = mybir.ActivationFunctionType

P = 128
PACK = 4
D, T, I, Q = 512, 1024, 512, 128
BANK = 512
HALF = I // 2
HALF_COLS = HALF // 16

FLOPS = 2 * 2 * D * Q * T


def tile_attend_opengate_parts_kernel(tc, query, query2, keys_words, keys_scales, tags_words, tags_scales,
                                       thr, slope, offs, offs2, offs3, offs4, out):
    nc = tc.nc
    with ExitStack() as ctx:
        sb = ctx.enter_context(tc.tile_pool(name="sb", bufs=1))
        psum = ctx.enter_context(tc.psum_pool(name="psum", bufs=1))

        key_scale = sb.tile([P, T], U8, align_bytes=64)
        tag_scale = sb.tile([P, T], U8, align_bytes=64)
        f1 = sb.tile([P, T], F32)
        f2 = sb.tile([P, T], F32)
        nc.vector.memset(f1[:], 0.0)
        nc.vector.memset(f2[:], 0.0)

        warm_in = sb.tile([P, 1], F32)
        warm_out = sb.tile([P, 1], F32)
        nc.gpsimd.memset(warm_in[:], 0.0)
        nc.scalar.activation(out=warm_out[:], in_=warm_in[:], func=ACT.Sigmoid)
        raw = [sb.tile([P, PACK, Q], F32, name="raw%d" % u) for u in range(2)]
        key_words = [sb.tile([P, BANK], U32, align_bytes=64, name="key_words%d" % h) for h in range(2)]
        tag_words = sb.tile([P, 2 * T], U8, align_bytes=64)
        lists = [sb.tile([P, I // 16], U16, name="list%d" % u) for u in range(4)]
        thr_sb = sb.tile([P, 1], F32)
        slope_sb = sb.tile([P, 1], F32)

        def scale_rows(eng, plane, src, quad):
            eng.dma_start(out=plane[32 * quad:32 * quad + 4, :].bitcast(I32), in_=src[0, 4 * quad:4 * quad + 4, :].bitcast(I32))

        nc.sync.dma_start(out=raw[1][:], in_=query2.rearrange("(p j) c -> p j c", j=PACK))
        for quad in range(4):
            scale_rows(nc.sync, tag_scale, tags_scales, quad)
        nc.sync.dma_start(out=tag_words[:].bitcast(I32), in_=tags_words[0].bitcast(I32))
        nc.sync.dma_start(out=raw[0][:], in_=query.rearrange("(p j) c -> p j c", j=PACK))
        key_src = keys_words[0].rearrange("p n t -> p (n t)").bitcast(I32)
        nc.sync.dma_start(out=key_words[0][:].bitcast(I32), in_=key_src[:, :BANK])
        for quad in range(4):
            scale_rows(nc.sync, key_scale, keys_scales, quad)
        nc.sync.dma_start(out=key_words[1][:].bitcast(I32), in_=key_src[:, BANK:])
        for tile, src in zip(lists, (offs, offs2, offs3, offs4)):
            nc.sync.dma_start(tile[:], src)
        nc.sync.dma_start(out=thr_sb[:], in_=thr)
        nc.sync.dma_start(out=slope_sb[:], in_=slope)

        codes = {}
        scales = {}
        for u in (1, 0):
            grouped = sb.tile([P, Q, PACK], BF16, align_bytes=64, name="grouped%d" % u)
            nc.vector.tensor_copy(out=grouped[:].rearrange("p (c i) t -> p c t i", i=4),
                                  in_=raw[u][:].rearrange("p t (c i) -> p c t i", i=4))
            q_codes = sb.tile([P, Q], U32, align_bytes=64, name="q_codes%d" % u)
            q_scale = sb.tile([P, Q], U8, align_bytes=64, name="q_scale%d" % u)
            nc.vector.quantize_mx(out=q_codes[:].bitcast(FP8X4), scales=q_scale[:], in_=grouped[:].rearrange("p c t -> p (c t)"))
            codes[u] = q_codes
            scales[u] = q_scale

        spans = [(0, 512), (512, 768), (768, 1024)]
        banks = [psum.tile([P, hi - lo], F32, name="bank%d" % lo) for lo, hi in spans]
        for bank, (lo, hi) in zip(banks, spans):
            nc.tensor.matmul_mx(out=bank[:], lhsT=codes[1][:].bitcast(FP8X4), lhsT_scale=scales[1][:],
                                rhs=tag_words[:, 2 * lo:2 * hi].bitcast(FP4X4), rhs_scale=tag_scale[:, lo:hi],
                                start=True, stop=False)
        for bank, (lo, hi) in zip(banks, spans):
            h = lo // BANK
            nc.tensor.matmul_mx(out=bank[:], lhsT=codes[0][:].bitcast(FP8X4), lhsT_scale=scales[0][:],
                                rhs=key_words[h][:, lo - h * BANK:hi - h * BANK].bitcast(FP8X4), rhs_scale=key_scale[:, lo:hi],
                                start=False, stop=True)

        a = sb.tile([P, T], F32)
        nc.scalar.copy(out=a[:, :512], in_=banks[0][:])
        nc.vector.tensor_copy(out=a[:, 512:768], in_=banks[1][:])
        nc.vector.tensor_copy(out=a[:, 768:], in_=banks[2][:])

        halves = [slice(h * HALF_COLS, (h + 1) * HALF_COLS) for h in range(2)]
        picked = sb.tile([P, I], F32)
        nc.vector.tensor_copy(out=picked[:, :HALF], in_=a[:].indirect(lists[0][:, halves[0]]))
        nc.scalar.activation(out=picked[:, HALF:], in_=a[:].indirect(lists[0][:, halves[1]]), func=ACT.Copy)
        nc.vector.tensor_copy(out=f1[:].indirect(lists[1][:]), in_=picked[:])
        cc = sb.tile([P, T], F32)
        nc.gpsimd.tensor_tensor(out=cc[:, 704:], in0=a[:, 704:], in1=f1[:, 704:], op=ALU.add)
        nc.vector.tensor_tensor(out=cc[:, :512], in0=banks[0][:], in1=f1[:, :512], op=ALU.add)
        nc.vector.tensor_tensor(out=cc[:, 512:704], in0=banks[1][:, :192], in1=f1[:, 512:704], op=ALU.add)

        gate = [sb.tile([P, HALF], F32, name="gate%d" % h) for h in range(2)]
        for h in range(2):
            nc.scalar.activation(out=gate[h][:], in_=cc[:].indirect(lists[2][:, halves[h]]), func=ACT.Sigmoid,
                                 bias=thr_sb[:], scale=slope_sb[:])
        for h in range(2):
            nc.vector.tensor_copy(out=f2[:].indirect(lists[0][:, halves[h]]), in_=gate[h][:])
        dd = sb.tile([P, T], F32)
        nc.vector.scalar_tensor_tensor(out=dd[:], in0=f2[:], scalar=-2.0, in1=cc[:], op0=ALU.mult, op1=ALU.add)

        result = [sb.tile([P, HALF], F32, name="result%d" % h) for h in range(2)]
        nc.vector.tensor_copy(out=result[0][:], in_=dd[:].indirect(lists[3][:, halves[0]]))
        nc.scalar.activation(out=result[1][:], in_=dd[:].indirect(lists[3][:, halves[1]]), func=ACT.Copy)
        nc.sync.dma_start(out=out[:, :HALF], in_=result[0][:])
        nc.scalar.dma_start(out=out[:, HALF:], in_=result[1][:])
